import numpy as np, ml_dtypes
CORES = [8,9,10,11,12,13]
N = 6
import mx_ref
BF = ml_dtypes.bfloat16
def entries(a):
    return np.ascontiguousarray(a.T).reshape(-1)
def table(e):
    return np.ascontiguousarray(np.reshape(e, (-1, 16)).T).astype(np.int32)
def cols(t, e):
    v = np.concatenate([t.reshape(128, -1, 4), np.zeros((128, 1, 4), BF)], axis=1)
    return np.ascontiguousarray(v[:, e]).reshape(128, -1)
def tile(rs):
    return np.stack(rs, axis=2).reshape(128, -1).astype(BF)
def f(rng, *shape):
    return mx_ref.flush((rng.standard_normal(shape, dtype=np.float32) * np.exp2(rng.integers(-2, 3, shape[:-1] + (1,)))).astype(BF))
def wide(rng, *shape, cols=0):
    v = rng.standard_normal(shape, dtype=np.float32) * np.exp2(rng.integers(-12, 13, shape)).astype(np.float32)
    if cols: v *= np.repeat(np.exp2(rng.integers(-cols, cols + 1, shape[:-2] + (1, shape[-1] // 4))) * (rng.random(shape[:-2] + (1, shape[-1] // 4)) > 0.0625), 4, axis=-1).astype(np.float32)
    return mx_ref.flush(v.astype(BF))
T, E, EC, CAPP = 256, 4, 128, 64
def lists(rng, case=""):
    sn, so = np.full((N, N, CAPP), -1), np.full((N, E, EC), -1)
    lone = rng.integers(0, N)
    for d in range(N):
        a = rng.integers(0, E)
        n = rng.integers(CAPP // 4, CAPP + 1, N)
        if case == "full": n[:] = CAPP
        if case == "empty": n[(d + 1) % N] = 0
        if case == "empty" and d == lone: n[np.arange(N) != d] = 0
        used = np.concatenate([s * CAPP + (np.arange(n[s]) if case == "sorted" else rng.permutation(CAPP)[:n[s]]) for s in range(N)])
        if case == "one": used = rng.permutation(N * CAPP)[:EC + rng.integers(E - 1, 8 * E - 7)]
        if case != "sorted": used = rng.permutation(used)
        if case == "empty": used = used[:(E - 1) * EC]
        key = rng.random((E, EC)) * np.exp2(rng.integers(-1, 2, (E, 1)))
        if case in ("full", "one"): key[a] = -1
        if case == "empty": key[a] = 9
        who = np.argsort(key.reshape(-1))[:len(used)] // EC
        if case == "sorted": who = np.sort(who)
        for m in range(E):
            k = used[who == m]; so[d, m, :len(k)] = k
        sn[used // CAPP, d, used % CAPP] = rng.integers(0, T, len(used))
        if case == "sorted":
            for s in range(N): sn[s, d, :n[s]] = np.sort(sn[s, d, :n[s]])
    return {"sn": np.stack([table(q) for q in sn]), "so": np.stack([table(q) for q in so])}
def setup_inputs(rng):
    return {"x": f(rng, N, 128, 4 * T), "w": f(rng, N, 128, 2048 * E), "v": f(rng, N, 128, 512 * E), **lists(rng)}
def setup_inputs_full(rng):
    return {**setup_inputs(rng), **lists(rng, "full")}
def setup_inputs_one(rng):
    return {**setup_inputs(rng), **lists(rng, "one")}
def setup_inputs_empty(rng):
    return {**setup_inputs(rng), **lists(rng, "empty")}
def setup_inputs_sorted(rng):
    return {**setup_inputs(rng), **lists(rng, "sorted")}
def setup_inputs_spread(rng):
    d = setup_inputs(rng); d["x"] = wide(rng, N, 128, 4 * T, cols=6); return d
def check_inputs(d):
    b = []
    for r in range(N):
        c, e = entries(d["sn"][r]), entries(d["so"][r]).reshape(E, EC)
        if c.min() < -1 or c.max() >= T: b.append("sn")
        got = np.concatenate([entries(d["sn"][s])[r * CAPP:(r + 1) * CAPP] for s in range(N)])
        if e.min() < -1 or ((e[:, 1:] >= 0) & (e[:, :-1] < 0)).any() or np.sort(e[e >= 0]).tolist() != np.flatnonzero(got >= 0).tolist(): b.append("so")
    return b
def reference(x, w, v, sn, so):
    y = np.zeros((N, 128, E * EC), np.float32)
    for r in range(N):
        arrived = np.concatenate([cols(x[s], entries(sn[s])[r * CAPP:(r + 1) * CAPP]) for s in range(N)], axis=1)
        e = entries(so[r])
        for m in range(E):
            k = e[EC * m:EC * m + EC]
            t = mx_ref.quantize(cols(arrived, k))
            R = []
            for i in range(4):
                W = mx_ref.quantize(np.ascontiguousarray(w[r][:, 2048 * m + 512 * i:2048 * m + 512 * i + 512]))
                R.append(np.maximum(mx_ref.matmul(W, t), np.float32(0)) * np.float32(0.05))
            z = mx_ref.matmul(mx_ref.quantize(np.ascontiguousarray(v[r][:, 512 * m:512 * m + 512])), mx_ref.quantize(tile(R)))
            y[r][:, EC * m:EC * m + EC] = np.where(k >= 0, z, np.float32(0))
    return {"y": y}

@@ -1,0 +1,239 @@
+import numpy as np
+from concourse.bass import DstId, RemoteDMATransfer
+from concourse.mybir import dt, AluOpType, ActivationFunctionType
+
+N, E, EC, CAPP, TOK = 6, 4, 128, 64, 256
+ZC = 128
+LW = ZC + N * CAPP
+KS = CAPP // 16
+KE = EC // 16
+
+SCRATCH = {
+    "xt": ("sbuf", [128, 4 * TOK], "bfloat16"),
+    "wt": ("sbuf", [128, 2048 * E], "bfloat16"),
+    "vt": ("sbuf", [128, 512 * E], "bfloat16"),
+    "zt": ("sbuf", [128, 4 * ZC], "bfloat16"),
+    "snl": ("sbuf", [128, N * KS], "int32"),
+    "sol": ("sbuf", [128, E * KE], "int32"),
+    "offn": ("sbuf", [128, N * KS], "uint16"),
+    "offo": ("sbuf", [128, E * KE], "uint16"),
+    "xq": ("sbuf", [128, TOK], "float8_e4m3fn_x4"),
+    "xs": ("sbuf", [128, TOK], "uint8"),
+    "slot": ("sbuf", [128, (N - 1) * CAPP], "float8_e4m3fn_x4"),
+    "slots": ("sbuf", [128, (N - 1) * CAPP], "uint8"),
+    "land": ("sbuf", [128, LW], "float8_e4m3fn_x4"),
+    "lands": ("sbuf", [128, LW], "uint8"),
+    "grp": ("sbuf", [128, E * EC], "float8_e4m3fn_x4"),
+    "grps": ("sbuf", [128, E * EC], "uint8"),
+    "wq": ("sbuf", [128, 512 * E], "float8_e4m3fn_x4"),
+    "ws": ("sbuf", [128, 512 * E], "uint8"),
+    "vq": ("sbuf", [128, 128 * E], "float8_e4m3fn_x4"),
+    "vs": ("sbuf", [128, 128 * E], "uint8"),
+    "h": ("sbuf", [128, 512 * E], "bfloat16"),
+    "hq": ("sbuf", [128, EC * E], "float8_e4m3fn_x4"),
+    "hs": ("sbuf", [128, EC * E], "uint8"),
+    "yo": ("sbuf", [128, EC * E], "float32"),
+    "ps": ("psum", [128, 4096], "float32"),
+}
+SEMAPHORES = (["lx", "ln", "lo", "lw0", "lw3", "lv", "zf", "zq", "xqd", "cn", "co", "pc", "pscl", "oc", "oscl",
+               "sent", "arrc", "arrs", "rel", "ya", "yb", "sta", "stb"]
+              + ["%s%d" % (n, m) for n in ("gc", "gs", "wq", "qv", "ev", "qh", "mv") for m in range(E)]
+              + ["mm%d%d" % (m, b) for m in range(E) for b in range(4)])
+
+LOADS_SYNC = "x n0 n1 n2 w02".split()
+LOADS_SCALAR = "n3 n4 n5 n6 n7 o0 o1 o2 o3 o4 o5 o6 o7".split()
+LOADS_LATE = "w33 v".split()
+ORDER_V = "w0 o w1 w2 p0 p1 p2 p3 s2 e00 e01 e03 w3 e12 e21 q0 q1 v01 v22 q2 e33 v33 q3".split()
+ORDER_A = "s0 s1 s3 e02 e10 e11 e13 e20 e22 e23 e31 e32 e30 y0 y1 y2 y3".split()
+ORDER_P = "w0 w1 w2 w3 v0 v1 v2 v3".split()
+
+
+def plan(core, others, topo):
+    far = [d for d in others if topo.die(d) != topo.die(core)]
+    near = [d for d in others if topo.die(d) == topo.die(core)]
+    order = near[:1] + far + near[1:]
+    out = []
+    for first, turn in ((1, 0), (0, 2)):
+        masks = {}
+        for i, dst in enumerate(order):
+            eng = topo.engines(core, dst)
+            wide, narrow = eng[first::2], eng[1 - first::2]
+            k = 2 * ((i - 1 + turn) % 4)
+            mine = wide if i == 0 else narrow[k:k + 2]
+            masks[dst] = (sum(1 << e for e in mine), len(mine))
+        out.append(masks)
+    return out
+
+
+def rank_program(g, core, T, topo):
+    r = T.rank_of(core)
+    if r is None:
+        return
+    S = T.sem
+    V, A, P, Y = g.vector, g.scalar, g.tensor, g.sync
+    Copy, Relu = ActivationFunctionType.Copy, ActivationFunctionType.Relu
+    ring = [(r + 1 + i) % N for i in range(N - 1)]
+    plans = {s: plan(T.cores[s], [T.cores[(s + 1 + i) % N] for i in range(N - 1)], topo) for s in range(N)}
+    load_of, part_of = {}, {}
+    for t in LOADS_SYNC + LOADS_LATE:
+        if t[0] == "w":
+            load_of.update({m: S["lw" + t[1]] for m in range(int(t[1]), int(t[2]) + 1)})
+    for t in ORDER_V:
+        if t[0] == "v":
+            part_of.update({m: S["qv" + t[1]] for m in range(int(t[1]), int(t[2]) + 1)})
+
+    def load(q, t):
+        if t[0] == "x":
+            q.dma_start(T.xt[:], T.x[:]).then_inc(S.lx, 16)
+        elif t[0] in "no":
+            k = 16 * int(t[1])
+            dst, src, s = (T.snl, T.sn, S.ln) if t[0] == "n" else (T.sol, T.so, S.lo)
+            q.dma_start(dst[k:k + 16, :], src[:]).then_inc(s, 16)
+        elif t[0] == "w":
+            a, b = 2048 * int(t[1]), 2048 * (int(t[2]) + 1)
+            q.dma_start(T.wt[:, a:b], T.w[:, a:b]).then_inc(S["lw" + t[1]], 16)
+        elif t[0] == "v":
+            q.dma_start(T.vt[:], T.v[:]).then_inc(S.lv, 16)
+
+    for t in LOADS_SYNC:
+        load(Y, t)
+    for t in LOADS_SCALAR:
+        load(A, t)
+
+    V.memset(T.zt[:], 0.0).then_inc(S.zf, 1)
+    V.wait_ge(S.zf, 1)
+    V.quantize_mx(T.land[:, 0:ZC], T.lands[:, 0:ZC], T.zt[:]).then_inc(S.zq, 1)
+    V.wait_ge(S.lx, 16)
+    V.quantize_mx(T.xq[:], T.xs[:], T.xt[:]).then_inc(S.xqd, 1)
+    V.wait_ge(S.ln, 128)
+    cut = KS * (r + 1)
+    V.tensor_copy(T.offn[:, N * KS - cut:N * KS], T.snl[:, 0:cut]).then_inc(S.cn, 1)
+    ncn = 1
+    if cut < N * KS:
+        V.tensor_copy(T.offn[:, 0:N * KS - cut], T.snl[:, cut:N * KS]).then_inc(S.cn, 1)
+        ncn = 2
+    nk = (N - 1) * KS
+    mine = slice(ZC + CAPP * r, ZC + CAPP * (r + 1))
+    V.wait_ge(S.xqd, 1)
+    V.wait_ge(S.cn, ncn)
+    V.tensor_copy(T.slot[:].bitcast(dt.uint32), T.xq[:].bitcast(dt.uint32).indirect(T.offn[:, 0:nk])).then_inc(S.pc, 1)
+    V.tensor_copy(T.land[:, mine].bitcast(dt.uint32), T.xq[:].bitcast(dt.uint32).indirect(T.offn[:, nk:nk + KS])).then_inc(S.oc, 1)
+
+    A.wait_ge(S.xqd, 1)
+    A.wait_ge(S.cn, ncn)
+    A.activation(T.slots[:], T.xs[:].indirect(T.offn[:, 0:nk]), Copy).then_inc(S.pscl, 1)
+    A.activation(T.lands[:, mine], T.xs[:].indirect(T.offn[:, nk:nk + KS]), Copy).then_inc(S.oscl, 1)
+
+    def send(kind, src, dst, remote_sem):
+        transfers = []
+        for i, d in enumerate(ring):
+            to = T.cores[d]
+            rid, pid = topo.addr(to)[:2]
+            a, b = src[:, CAPP * i:CAPP * (i + 1)], dst[:, mine]
+            if kind == 0:
+                a, b = a.bitcast(dt.uint8), b.bitcast(dt.uint8)
+            transfers.append(RemoteDMATransfer(dst_ids=[DstId(rid=rid, pnc=pid)], dma_engine_mask=plans[r][kind][to][0],
+                                               remote_sem=remote_sem, src=a, dst=b))
+        g.remote_dma_fused(transfers, local_sem=S.sent)
+
+    g.wait_ge(S.pc, 1)
+    send(0, T.slot, T.land, S.arrc)
+    g.wait_ge(S.pscl, 1)
+    send(1, T.slots, T.lands, S.arrs)
+    g.sem_inc(S.rel, 1)
+    g.wait_ge(S.sent, sum(n for p in plans[r] for _, n in p.values()))
+    here = [sum(plans[s][k][core][1] for s in range(N) if s != r) for k in (0, 1)]
+
+    Y.wait_ge(S.rel, 1)
+    for t in LOADS_LATE:
+        load(Y, t)
+
+    def offsets_so():
+        V.wait_ge(S.lo, 128)
+        V.tensor_scalar(T.offo[:], T.sol[:], ZC, None, AluOpType.add).then_inc(S.co, 1)
+
+    def quant_w(m):
+        V.wait_ge(load_of[m], 16)
+        V.quantize_mx(T.wq[:, 512 * m:512 * m + 512], T.ws[:, 512 * m:512 * m + 512],
+                      T.wt[:, 2048 * m:2048 * m + 2048]).then_inc(S["wq%d" % m], 1)
+
+    def quant_v(a, b):
+        V.wait_ge(S.lv, 16)
+        V.quantize_mx(T.vq[:, 128 * a:128 * b + 128], T.vs[:, 128 * a:128 * b + 128],
+                      T.vt[:, 512 * a:512 * b + 512]).then_inc(S["qv%d" % a], 1)
+
+    def pick_codes(m):
+        for s, n in ((S.zq, 1), (S.oc, 1), (S.co, 1), (S.arrc, here[0])):
+            V.wait_ge(s, n)
+        V.tensor_copy(T.grp[:, EC * m:EC * m + EC].bitcast(dt.uint32),
+                      T.land[:].bitcast(dt.uint32).indirect(T.offo[:, KE * m:KE * m + KE])).then_inc(S["gc%d" % m], 1)
+
+    def pick_scales(m, on_vector):
+        q = V if on_vector else A
+        for s, n in ((S.zq, 1), (S.oscl, 1), (S.co, 1), (S.arrs, here[1])):
+            q.wait_ge(s, n)
+        out, win = T.grps[:, EC * m:EC * m + EC], T.lands[:].indirect(T.offo[:, KE * m:KE * m + KE])
+        (V.tensor_copy(out, win) if on_vector else A.activation(out, win, Copy)).then_inc(S["gs%d" % m], 1)
+
+    def bank(m, b):
+        k = 512 * (4 * (m % 2) + b)
+        return T.ps[:, k:k + EC]
+
+    def evict(m, b, on_vector):
+        out, z = T.h[:, 512 * m + b:512 * m + 512:4], bank(m, b)
+        if on_vector:
+            V.wait_ge(S["mm%d%d" % (m, b)], 1)
+            V.tensor_scalar(out, z, 0.0, 0.05, AluOpType.max, AluOpType.mult).then_inc(S["ev%d" % m], 1)
+        else:
+            A.wait_ge(S["mm%d%d" % (m, b)], 1)
+            A.activation(out, z, Relu, scale=0.05).then_inc(S["ev%d" % m], 1)
+
+    def quant_h(m):
+        V.wait_ge(S["ev%d" % m], 4)
+        V.quantize_mx(T.hq[:, EC * m:EC * m + EC], T.hs[:, EC * m:EC * m + EC], T.h[:, 512 * m:512 * m + 512]).then_inc(S["qh%d" % m], 1)
+
+    def take_y(m, on_vector):
+        out, z = T.yo[:, EC * m:EC * m + EC], T.ps[:, 512 * m:512 * m + EC]
+        q = V if on_vector else A
+        q.wait_ge(S["mv%d" % m], 1)
+        (V.tensor_copy(out, z) if on_vector else A.activation(out, z, Copy)).then_inc(S["ya" if m < 2 else "yb"], 1)
+
+    def products_w(m):
+        for s in ("gc", "gs", "wq"):
+            P.wait_ge(S["%s%d" % (s, m)], 1)
+        if m >= 2:
+            P.wait_ge(S["ev%d" % (m - 2)], 4)
+        for b in range(4):
+            k = 512 * m + 128 * b
+            P.matmul_mx(bank(m, b), T.wq[:, k:k + 128], T.ws[:, k:k + 128],
+                        T.grp[:, EC * m:EC * m + EC], T.grps[:, EC * m:EC * m + EC], True, True).then_inc(S["mm%d%d" % (m, b)], 1)
+
+    def product_v(m):
+        if m == 0:
+            P.wait_ge(S.ev2, 4)
+        P.wait_ge(part_of[m], 1)
+        P.wait_ge(S["qh%d" % m], 1)
+        P.matmul_mx(T.ps[:, 512 * m:512 * m + EC], T.vq[:, 128 * m:128 * m + 128], T.vs[:, 128 * m:128 * m + 128],
+                    T.hq[:, EC * m:EC * m + EC], T.hs[:, EC * m:EC * m + EC], True, True).then_inc(S["mv%d" % m], 1)
+
+    for t in ORDER_V:
+        if t == "o": offsets_so()
+        elif t[0] == "w": quant_w(int(t[1]))
+        elif t[0] == "v": quant_v(int(t[1]), int(t[2]))
+        elif t[0] == "p": pick_codes(int(t[1]))
+        elif t[0] == "s": pick_scales(int(t[1]), True)
+        elif t[0] == "e": evict(int(t[1]), int(t[2]), True)
+        elif t[0] == "q": quant_h(int(t[1]))
+        elif t[0] == "y": take_y(int(t[1]), True)
+    for t in ORDER_A:
+        if t[0] == "s": pick_scales(int(t[1]), False)
+        elif t[0] == "e": evict(int(t[1]), int(t[2]), False)
+        elif t[0] == "y": take_y(int(t[1]), False)
+    for t in ORDER_P:
+        (products_w if t[0] == "w" else product_v)(int(t[1]))
+
+    for s, t, a in ((S.ya, S.sta, 0), (S.yb, S.stb, 2 * EC)):
+        Y.wait_ge(s, 2)
+        Y.dma_start(T.y[:, a:a + 2 * EC], T.yo[:, a:a + 2 * EC]).then_inc(t, 16)
+    Y.wait_ge(S.sta, 16)
+    Y.wait_ge(S.stb, 16)

@@ -35,16 +35,16 @@ SCRATCH = {
     "yo": ("sbuf", [128, EC * E], "float32"),
     "ps": ("psum", [128, 4096], "float32"),
 }
-SEMAPHORES = (["lx", "ln", "lo", "lw0", "lw3", "lv", "zf", "zq", "xqd", "cn", "co", "pc", "pscl", "oc", "oscl",
-               "sent", "arrc", "arrs", "rel", "ya", "yb", "sta", "stb"]
-              + ["%s%d" % (n, m) for n in ("gc", "gs", "wq", "qv", "ev", "qh", "mv") for m in range(E)]
+SEMAPHORES = (["lx", "ln", "lo", "lv", "zf", "zq", "xqd", "cn", "co", "pc", "pscl", "oc", "oscl",
+               "sent", "arrc", "arrs", "ya", "yb", "sta", "stb"]
+              + ["%s%d" % (n, m) for n in ("gc", "gs", "lw", "wq", "qv", "ev", "qh", "mv") for m in range(E)]
               + ["mm%d%d" % (m, b) for m in range(E) for b in range(4)])
 
-LOADS_SYNC = "x n0 n1 n2 w02".split()
-LOADS_SCALAR = "n3 n4 n5 n6 n7 o0 o1 o2 o3 o4 o5 o6 o7".split()
-LOADS_LATE = "w33 v".split()
-ORDER_V = "w0 o w1 w2 p0 p1 p2 p3 s2 e00 e01 e03 w3 e12 e21 q0 q1 v01 v22 q2 e33 v33 q3".split()
-ORDER_A = "s0 s1 s3 e02 e10 e11 e13 e20 e22 e23 e31 e32 e30 y0 y1 y2 y3".split()
+LOADS_SYNC = "x n0 n1 n2 o0 o1 o2 o3 w00 w11 w22".split()
+LOADS_SCALAR = "n3 n4 n5 n6 n7 o4 o5 o6 o7".split()
+LOADS_MID = "w33 v".split()
+ORDER_V = "w0 w1 o w2 w3 v03 p0 p1 p2 p3 s2 e02 e03 e12 e13 q0 q1 e21 e30 q2 e33 q3 y0 y3".split()
+ORDER_A = "s0 s1 s3 e01 e00 e11 e10 e20 e22 e23 e31 e32 y1 y2".split()
 ORDER_P = "w0 w1 w2 w3 v0 v1 v2 v3".split()
 
 
@@ -74,13 +74,14 @@ def rank_program(g, core, T, topo):
     Copy, Relu = ActivationFunctionType.Copy, ActivationFunctionType.Relu
     ring = [(r + 1 + i) % N for i in range(N - 1)]
     plans = {s: plan(T.cores[s], [T.cores[(s + 1 + i) % N] for i in range(N - 1)], topo) for s in range(N)}
-    load_of, part_of = {}, {}
-    for t in LOADS_SYNC + LOADS_LATE:
-        if t[0] == "w":
-            load_of.update({m: S["lw" + t[1]] for m in range(int(t[1]), int(t[2]) + 1)})
-    for t in ORDER_V:
-        if t[0] == "v":
-            part_of.update({m: S["qv" + t[1]] for m in range(int(t[1]), int(t[2]) + 1)})
+
+    def by_expert(tokens, kind, sem):
+        return {m: S[sem + t[1]] for t in tokens if t[0] == kind for m in range(int(t[1]), int(t[-1]) + 1)}
+
+    load_of = by_expert(LOADS_SYNC + LOADS_MID, "w", "lw")
+    part_of = by_expert(ORDER_V, "v", "qv")
+    codes_of = by_expert(ORDER_V, "p", "gc")
+    scales_of = by_expert(ORDER_V + ORDER_A, "s", "gs")
 
     def load(q, t):
         if t[0] == "x":
@@ -99,6 +100,9 @@ def rank_program(g, core, T, topo):
         load(Y, t)
     for t in LOADS_SCALAR:
         load(A, t)
+    Y.wait_ge(S.lx, 16)
+    for t in LOADS_MID:
+        load(Y, t)
 
     V.memset(T.zt[:], 0.0).then_inc(S.zf, 1)
     V.wait_ge(S.zf, 1)
@@ -140,13 +144,8 @@ def rank_program(g, core, T, topo):
     send(0, T.slot, T.land, S.arrc)
     g.wait_ge(S.pscl, 1)
     send(1, T.slots, T.lands, S.arrs)
-    g.sem_inc(S.rel, 1)
     g.wait_ge(S.sent, sum(n for p in plans[r] for _, n in p.values()))
     here = [sum(plans[s][k][core][1] for s in range(N) if s != r) for k in (0, 1)]
-
-    Y.wait_ge(S.rel, 1)
-    for t in LOADS_LATE:
-        load(Y, t)
 
     def offsets_so():
         V.wait_ge(S.lo, 128)
@@ -162,18 +161,18 @@ def rank_program(g, core, T, topo):
         V.quantize_mx(T.vq[:, 128 * a:128 * b + 128], T.vs[:, 128 * a:128 * b + 128],
                       T.vt[:, 512 * a:512 * b + 512]).then_inc(S["qv%d" % a], 1)
 
-    def pick_codes(m):
+    def pick_codes(a, b):
         for s, n in ((S.zq, 1), (S.oc, 1), (S.co, 1), (S.arrc, here[0])):
             V.wait_ge(s, n)
-        V.tensor_copy(T.grp[:, EC * m:EC * m + EC].bitcast(dt.uint32),
-                      T.land[:].bitcast(dt.uint32).indirect(T.offo[:, KE * m:KE * m + KE])).then_inc(S["gc%d" % m], 1)
+        V.tensor_copy(T.grp[:, EC * a:EC * b + EC].bitcast(dt.uint32),
+                      T.land[:].bitcast(dt.uint32).indirect(T.offo[:, KE * a:KE * b + KE])).then_inc(S["gc%d" % a], 1)
 
-    def pick_scales(m, on_vector):
+    def pick_scales(a, b, on_vector):
         q = V if on_vector else A
         for s, n in ((S.zq, 1), (S.oscl, 1), (S.co, 1), (S.arrs, here[1])):
             q.wait_ge(s, n)
-        out, win = T.grps[:, EC * m:EC * m + EC], T.lands[:].indirect(T.offo[:, KE * m:KE * m + KE])
-        (V.tensor_copy(out, win) if on_vector else A.activation(out, win, Copy)).then_inc(S["gs%d" % m], 1)
+        out, win = T.grps[:, EC * a:EC * b + EC], T.lands[:].indirect(T.offo[:, KE * a:KE * b + KE])
+        (V.tensor_copy(out, win) if on_vector else A.activation(out, win, Copy)).then_inc(S["gs%d" % a], 1)
 
     def bank(m, b):
         k = 512 * (4 * (m % 2) + b)
@@ -199,8 +198,8 @@ def rank_program(g, core, T, topo):
         (V.tensor_copy(out, z) if on_vector else A.activation(out, z, Copy)).then_inc(S["ya" if m < 2 else "yb"], 1)
 
     def products_w(m):
-        for s in ("gc", "gs", "wq"):
-            P.wait_ge(S["%s%d" % (s, m)], 1)
+        for s in (S["wq%d" % m], codes_of[m], scales_of[m]):
+            P.wait_ge(s, 1)
         if m >= 2:
             P.wait_ge(S["ev%d" % (m - 2)], 4)
         for b in range(4):
@@ -220,13 +219,13 @@ def rank_program(g, core, T, topo):
         if t == "o": offsets_so()
         elif t[0] == "w": quant_w(int(t[1]))
         elif t[0] == "v": quant_v(int(t[1]), int(t[2]))
-        elif t[0] == "p": pick_codes(int(t[1]))
-        elif t[0] == "s": pick_scales(int(t[1]), True)
+        elif t[0] == "p": pick_codes(int(t[1]), int(t[-1]))
+        elif t[0] == "s": pick_scales(int(t[1]), int(t[-1]), True)
         elif t[0] == "e": evict(int(t[1]), int(t[2]), True)
         elif t[0] == "q": quant_h(int(t[1]))
         elif t[0] == "y": take_y(int(t[1]), True)
     for t in ORDER_A:
-        if t[0] == "s": pick_scales(int(t[1]), False)
+        if t[0] == "s": pick_scales(int(t[1]), int(t[-1]), False)
         elif t[0] == "e": evict(int(t[1]), int(t[2]), False)
         elif t[0] == "y": take_y(int(t[1]), False)
     for t in ORDER_P:

@@ -35,16 +35,16 @@ SCRATCH = {
     "yo": ("sbuf", [128, EC * E], "float32"),
     "ps": ("psum", [128, 4096], "float32"),
 }
-SEMAPHORES = (["lx", "ln", "lo", "lv", "zf", "zq", "xqd", "cn", "co", "pc", "pscl", "oc", "oscl",
+SEMAPHORES = (["lx", "ln", "lo", "zf", "zq", "xqd", "cn", "co", "pc", "pscl", "oc", "oscl",
                "sent", "arrc", "arrs", "ya", "yb", "sta", "stb"]
-              + ["%s%d" % (n, m) for n in ("gc", "gs", "lw", "wq", "qv", "ev", "qh", "mv") for m in range(E)]
+              + ["%s%d" % (n, m) for n in ("gc", "gs", "lw", "lv", "wq", "qv", "ev", "qh", "mv") for m in range(E)]
               + ["mm%d%d" % (m, b) for m in range(E) for b in range(4)])
 
-LOADS_SYNC = "x n0 n1 n2 o0 o1 o2 o3 w00 w11 w22".split()
+LOADS_SYNC = "x n0 n1 n2 o0 o1 o2 o3 w0 w1 w2".split()
 LOADS_SCALAR = "n3 n4 n5 n6 n7 o4 o5 o6 o7".split()
-LOADS_MID = "w33 v".split()
-ORDER_V = "w0 w1 o w2 w3 v03 p0 p1 p2 p3 s2 e02 e03 e12 e13 q0 q1 e21 e30 q2 e33 q3 y0 y3".split()
-ORDER_A = "s0 s1 s3 e01 e00 e11 e10 e20 e22 e23 e31 e32 y1 y2".split()
+LOADS_LATE = "w3 v01 v23".split()
+ORDER_V = "w0 o w1 w2 p0 p1 p2 p3 e02 e03 e12 e11 w3 e23 e21 q0 v01 e30 v23 q1 q2 q3 y0 y3".split()
+ORDER_A = "s0 s1 s2 s3 e01 e00 e10 e13 e22 e20 e32 e33 e31 y1 y2".split()
 ORDER_P = "w0 w1 w2 w3 v0 v1 v2 v3".split()
 
 
@@ -74,11 +74,13 @@ def rank_program(g, core, T, topo):
     Copy, Relu = ActivationFunctionType.Copy, ActivationFunctionType.Relu
     ring = [(r + 1 + i) % N for i in range(N - 1)]
     plans = {s: plan(T.cores[s], [T.cores[(s + 1 + i) % N] for i in range(N - 1)], topo) for s in range(N)}
+    left = sum(n for p in plans[r] for _, n in p.values())
 
     def by_expert(tokens, kind, sem):
         return {m: S[sem + t[1]] for t in tokens if t[0] == kind for m in range(int(t[1]), int(t[-1]) + 1)}
 
-    load_of = by_expert(LOADS_SYNC + LOADS_MID, "w", "lw")
+    wload_of = by_expert(LOADS_SYNC + LOADS_LATE, "w", "lw")
+    vload_of = by_expert(LOADS_SYNC + LOADS_LATE, "v", "lv")
     part_of = by_expert(ORDER_V, "v", "qv")
     codes_of = by_expert(ORDER_V, "p", "gc")
     scales_of = by_expert(ORDER_V + ORDER_A, "s", "gs")
@@ -90,18 +92,17 @@ def rank_program(g, core, T, topo):
             k = 16 * int(t[1])
             dst, src, s = (T.snl, T.sn, S.ln) if t[0] == "n" else (T.sol, T.so, S.lo)
             q.dma_start(dst[k:k + 16, :], src[:]).then_inc(s, 16)
-        elif t[0] == "w":
-            a, b = 2048 * int(t[1]), 2048 * (int(t[2]) + 1)
-            q.dma_start(T.wt[:, a:b], T.w[:, a:b]).then_inc(S["lw" + t[1]], 16)
-        elif t[0] == "v":
-            q.dma_start(T.vt[:], T.v[:]).then_inc(S.lv, 16)
+        else:
+            dst, src, k = (T.wt, T.w, 2048) if t[0] == "w" else (T.vt, T.v, 512)
+            a, b = k * int(t[1]), k * (int(t[-1]) + 1)
+            q.dma_start(dst[:, a:b], src[:, a:b]).then_inc(S["l" + t[:2]], 16)
 
     for t in LOADS_SYNC:
         load(Y, t)
     for t in LOADS_SCALAR:
         load(A, t)
-    Y.wait_ge(S.lx, 16)
-    for t in LOADS_MID:
+    Y.wait_ge(S.sent, left)
+    for t in LOADS_LATE:
         load(Y, t)
 
     V.memset(T.zt[:], 0.0).then_inc(S.zf, 1)
@@ -144,7 +145,6 @@ def rank_program(g, core, T, topo):
     send(0, T.slot, T.land, S.arrc)
     g.wait_ge(S.pscl, 1)
     send(1, T.slots, T.lands, S.arrs)
-    g.wait_ge(S.sent, sum(n for p in plans[r] for _, n in p.values()))
     here = [sum(plans[s][k][core][1] for s in range(N) if s != r) for k in (0, 1)]
 
     def offsets_so():
@@ -152,12 +152,12 @@ def rank_program(g, core, T, topo):
         V.tensor_scalar(T.offo[:], T.sol[:], ZC, None, AluOpType.add).then_inc(S.co, 1)
 
     def quant_w(m):
-        V.wait_ge(load_of[m], 16)
+        V.wait_ge(wload_of[m], 16)
         V.quantize_mx(T.wq[:, 512 * m:512 * m + 512], T.ws[:, 512 * m:512 * m + 512],
                       T.wt[:, 2048 * m:2048 * m + 2048]).then_inc(S["wq%d" % m], 1)
 
     def quant_v(a, b):
-        V.wait_ge(S.lv, 16)
+        V.wait_ge(vload_of[a], 16)
         V.quantize_mx(T.vq[:, 128 * a:128 * b + 128], T.vs[:, 128 * a:128 * b + 128],
                       T.vt[:, 512 * a:512 * b + 512]).then_inc(S["qv%d" % a], 1)
 

import numpy as np
from concourse.bass import DstId, RemoteDMATransfer
from concourse.mybir import dt, AluOpType, ActivationFunctionType

N, E, EC, CAPP, TOK = 6, 4, 128, 64, 256
ZC = 128
LW = ZC + N * CAPP
KS = CAPP // 16
KE = EC // 16

SCRATCH = {
    "xt": ("sbuf", [128, 4 * TOK], "bfloat16"),
    "wt": ("sbuf", [128, 2048 * E], "bfloat16"),
    "vt": ("sbuf", [128, 512 * E], "bfloat16"),
    "zt": ("sbuf", [128, 4 * ZC], "bfloat16"),
    "snl": ("sbuf", [128, N * KS], "int32"),
    "sol": ("sbuf", [128, E * KE], "int32"),
    "offn": ("sbuf", [128, N * KS], "uint16"),
    "offo": ("sbuf", [128, E * KE], "uint16"),
    "xq": ("sbuf", [128, TOK], "float8_e4m3fn_x4"),
    "xs": ("sbuf", [128, TOK], "uint8"),
    "slot": ("sbuf", [128, (N - 1) * CAPP], "float8_e4m3fn_x4"),
    "slots": ("sbuf", [128, (N - 1) * CAPP], "uint8"),
    "land": ("sbuf", [128, LW], "float8_e4m3fn_x4"),
    "lands": ("sbuf", [128, LW], "uint8"),
    "grp": ("sbuf", [128, E * EC], "float8_e4m3fn_x4"),
    "grps": ("sbuf", [128, E * EC], "uint8"),
    "wq": ("sbuf", [128, 512 * E], "float8_e4m3fn_x4"),
    "ws": ("sbuf", [128, 512 * E], "uint8"),
    "vq": ("sbuf", [128, 128 * E], "float8_e4m3fn_x4"),
    "vs": ("sbuf", [128, 128 * E], "uint8"),
    "h": ("sbuf", [128, 512 * E], "bfloat16"),
    "hq": ("sbuf", [128, EC * E], "float8_e4m3fn_x4"),
    "hs": ("sbuf", [128, EC * E], "uint8"),
    "yo": ("sbuf", [128, EC * E], "float32"),
    "ps": ("psum", [128, 4096], "float32"),
}
SEMAPHORES = (["lx", "ln", "lo", "zf", "zq", "xqd", "cn", "co", "pc", "pscl", "oc", "oscl",
               "sent", "arrc", "arrs", "ya", "yb", "sta", "stb"]
              + ["%s%d" % (n, m) for n in ("gc", "gs", "lw", "lv", "wq", "qv", "ev", "qh", "mv") for m in range(E)]
              + ["mm%d%d" % (m, b) for m in range(E) for b in range(4)])

LOADS_SYNC = "x n0 n1 n2 o0 o1 o2 o3 w0 w1 w2".split()
LOADS_SCALAR = "n3 n4 n5 n6 n7 o4 o5 o6 o7".split()
LOADS_LATE = "w3 v01 v23".split()
ORDER_V = "w0 o w1 w2 p0 p1 p2 p3 e02 e03 e12 e11 w3 e23 e21 q0 v01 e30 v23 q1 q2 q3 y0 y3".split()
ORDER_A = "s0 s1 s2 s3 e01 e00 e10 e13 e22 e20 e32 e33 e31 y1 y2".split()
ORDER_P = "w0 w1 w2 w3 v0 v1 v2 v3".split()


def plan(core, others, topo):
    far = [d for d in others if topo.die(d) != topo.die(core)]
    near = [d for d in others if topo.die(d) == topo.die(core)]
    order = near[:1] + far + near[1:]
    out = []
    for first, turn in ((1, 0), (0, 2)):
        masks = {}
        for i, dst in enumerate(order):
            eng = topo.engines(core, dst)
            wide, narrow = eng[first::2], eng[1 - first::2]
            k = 2 * ((i - 1 + turn) % 4)
            mine = wide if i == 0 else narrow[k:k + 2]
            masks[dst] = (sum(1 << e for e in mine), len(mine))
        out.append(masks)
    return out


def rank_program(g, core, T, topo):
    r = T.rank_of(core)
    if r is None:
        return
    S = T.sem
    V, A, P, Y = g.vector, g.scalar, g.tensor, g.sync
    Copy, Relu = ActivationFunctionType.Copy, ActivationFunctionType.Relu
    ring = [(r + 1 + i) % N for i in range(N - 1)]
    plans = {s: plan(T.cores[s], [T.cores[(s + 1 + i) % N] for i in range(N - 1)], topo) for s in range(N)}
    left = sum(n for p in plans[r] for _, n in p.values())

    def by_expert(tokens, kind, sem):
        return {m: S[sem + t[1]] for t in tokens if t[0] == kind for m in range(int(t[1]), int(t[-1]) + 1)}

    wload_of = by_expert(LOADS_SYNC + LOADS_LATE, "w", "lw")
    vload_of = by_expert(LOADS_SYNC + LOADS_LATE, "v", "lv")
    part_of = by_expert(ORDER_V, "v", "qv")
    codes_of = by_expert(ORDER_V, "p", "gc")
    scales_of = by_expert(ORDER_V + ORDER_A, "s", "gs")

    def load(q, t):
        if t[0] == "x":
            q.dma_start(T.xt[:], T.x[:]).then_inc(S.lx, 16)
        elif t[0] in "no":
            k = 16 * int(t[1])
            dst, src, s = (T.snl, T.sn, S.ln) if t[0] == "n" else (T.sol, T.so, S.lo)
            q.dma_start(dst[k:k + 16, :], src[:]).then_inc(s, 16)
        else:
            dst, src, k = (T.wt, T.w, 2048) if t[0] == "w" else (T.vt, T.v, 512)
            a, b = k * int(t[1]), k * (int(t[-1]) + 1)
            q.dma_start(dst[:, a:b], src[:, a:b]).then_inc(S["l" + t[:2]], 16)

    for t in LOADS_SYNC:
        load(Y, t)
    for t in LOADS_SCALAR:
        load(A, t)
    Y.wait_ge(S.sent, left)
    for t in LOADS_LATE:
        load(Y, t)

    V.memset(T.zt[:], 0.0).then_inc(S.zf, 1)
    V.wait_ge(S.zf, 1)
    V.quantize_mx(T.land[:, 0:ZC], T.lands[:, 0:ZC], T.zt[:]).then_inc(S.zq, 1)
    V.wait_ge(S.lx, 16)
    V.quantize_mx(T.xq[:], T.xs[:], T.xt[:]).then_inc(S.xqd, 1)
    V.wait_ge(S.ln, 128)
    cut = KS * (r + 1)
    V.tensor_copy(T.offn[:, N * KS - cut:N * KS], T.snl[:, 0:cut]).then_inc(S.cn, 1)
    ncn = 1
    if cut < N * KS:
        V.tensor_copy(T.offn[:, 0:N * KS - cut], T.snl[:, cut:N * KS]).then_inc(S.cn, 1)
        ncn = 2
    nk = (N - 1) * KS
    mine = slice(ZC + CAPP * r, ZC + CAPP * (r + 1))
    V.wait_ge(S.xqd, 1)
    V.wait_ge(S.cn, ncn)
    V.tensor_copy(T.slot[:].bitcast(dt.uint32), T.xq[:].bitcast(dt.uint32).indirect(T.offn[:, 0:nk])).then_inc(S.pc, 1)
    V.tensor_copy(T.land[:, mine].bitcast(dt.uint32), T.xq[:].bitcast(dt.uint32).indirect(T.offn[:, nk:nk + KS])).then_inc(S.oc, 1)

    A.wait_ge(S.xqd, 1)
    A.wait_ge(S.cn, ncn)
    A.activation(T.slots[:], T.xs[:].indirect(T.offn[:, 0:nk]), Copy).then_inc(S.pscl, 1)
    A.activation(T.lands[:, mine], T.xs[:].indirect(T.offn[:, nk:nk + KS]), Copy).then_inc(S.oscl, 1)

    def send(kind, src, dst, remote_sem):
        transfers = []
        for i, d in enumerate(ring):
            to = T.cores[d]
            rid, pid = topo.addr(to)[:2]
            a, b = src[:, CAPP * i:CAPP * (i + 1)], dst[:, mine]
            if kind == 0:
                a, b = a.bitcast(dt.uint8), b.bitcast(dt.uint8)
            transfers.append(RemoteDMATransfer(dst_ids=[DstId(rid=rid, pnc=pid)], dma_engine_mask=plans[r][kind][to][0],
                                               remote_sem=remote_sem, src=a, dst=b))
        g.remote_dma_fused(transfers, local_sem=S.sent)

    g.wait_ge(S.pc, 1)
    send(0, T.slot, T.land, S.arrc)
    g.wait_ge(S.pscl, 1)
    send(1, T.slots, T.lands, S.arrs)
    here = [sum(plans[s][k][core][1] for s in range(N) if s != r) for k in (0, 1)]

    def offsets_so():
        V.wait_ge(S.lo, 128)
        V.tensor_scalar(T.offo[:], T.sol[:], ZC, None, AluOpType.add).then_inc(S.co, 1)

    def quant_w(m):
        V.wait_ge(wload_of[m], 16)
        V.quantize_mx(T.wq[:, 512 * m:512 * m + 512], T.ws[:, 512 * m:512 * m + 512],
                      T.wt[:, 2048 * m:2048 * m + 2048]).then_inc(S["wq%d" % m], 1)

    def quant_v(a, b):
        V.wait_ge(vload_of[a], 16)
        V.quantize_mx(T.vq[:, 128 * a:128 * b + 128], T.vs[:, 128 * a:128 * b + 128],
                      T.vt[:, 512 * a:512 * b + 512]).then_inc(S["qv%d" % a], 1)

    def pick_codes(a, b):
        for s, n in ((S.zq, 1), (S.oc, 1), (S.co, 1), (S.arrc, here[0])):
            V.wait_ge(s, n)
        V.tensor_copy(T.grp[:, EC * a:EC * b + EC].bitcast(dt.uint32),
                      T.land[:].bitcast(dt.uint32).indirect(T.offo[:, KE * a:KE * b + KE])).then_inc(S["gc%d" % a], 1)

    def pick_scales(a, b, on_vector):
        q = V if on_vector else A
        for s, n in ((S.zq, 1), (S.oscl, 1), (S.co, 1), (S.arrs, here[1])):
            q.wait_ge(s, n)
        out, win = T.grps[:, EC * a:EC * b + EC], T.lands[:].indirect(T.offo[:, KE * a:KE * b + KE])
        (V.tensor_copy(out, win) if on_vector else A.activation(out, win, Copy)).then_inc(S["gs%d" % a], 1)

    def bank(m, b):
        k = 512 * (4 * (m % 2) + b)
        return T.ps[:, k:k + EC]

    def evict(m, b, on_vector):
        out, z = T.h[:, 512 * m + b:512 * m + 512:4], bank(m, b)
        if on_vector:
            V.wait_ge(S["mm%d%d" % (m, b)], 1)
            V.tensor_scalar(out, z, 0.0, 0.05, AluOpType.max, AluOpType.mult).then_inc(S["ev%d" % m], 1)
        else:
            A.wait_ge(S["mm%d%d" % (m, b)], 1)
            A.activation(out, z, Relu, scale=0.05).then_inc(S["ev%d" % m], 1)

    def quant_h(m):
        V.wait_ge(S["ev%d" % m], 4)
        V.quantize_mx(T.hq[:, EC * m:EC * m + EC], T.hs[:, EC * m:EC * m + EC], T.h[:, 512 * m:512 * m + 512]).then_inc(S["qh%d" % m], 1)

    def take_y(m, on_vector):
        out, z = T.yo[:, EC * m:EC * m + EC], T.ps[:, 512 * m:512 * m + EC]
        q = V if on_vector else A
        q.wait_ge(S["mv%d" % m], 1)
        (V.tensor_copy(out, z) if on_vector else A.activation(out, z, Copy)).then_inc(S["ya" if m < 2 else "yb"], 1)

    def products_w(m):
        for s in (S["wq%d" % m], codes_of[m], scales_of[m]):
            P.wait_ge(s, 1)
        if m >= 2:
            P.wait_ge(S["ev%d" % (m - 2)], 4)
        for b in range(4):
            k = 512 * m + 128 * b
            P.matmul_mx(bank(m, b), T.wq[:, k:k + 128], T.ws[:, k:k + 128],
                        T.grp[:, EC * m:EC * m + EC], T.grps[:, EC * m:EC * m + EC], True, True).then_inc(S["mm%d%d" % (m, b)], 1)

    def product_v(m):
        if m == 0:
            P.wait_ge(S.ev2, 4)
        P.wait_ge(part_of[m], 1)
        P.wait_ge(S["qh%d" % m], 1)
        P.matmul_mx(T.ps[:, 512 * m:512 * m + EC], T.vq[:, 128 * m:128 * m + 128], T.vs[:, 128 * m:128 * m + 128],
                    T.hq[:, EC * m:EC * m + EC], T.hs[:, EC * m:EC * m + EC], True, True).then_inc(S["mv%d" % m], 1)

    for t in ORDER_V:
        if t == "o": offsets_so()
        elif t[0] == "w": quant_w(int(t[1]))
        elif t[0] == "v": quant_v(int(t[1]), int(t[2]))
        elif t[0] == "p": pick_codes(int(t[1]), int(t[-1]))
        elif t[0] == "s": pick_scales(int(t[1]), int(t[-1]), True)
        elif t[0] == "e": evict(int(t[1]), int(t[2]), True)
        elif t[0] == "q": quant_h(int(t[1]))
        elif t[0] == "y": take_y(int(t[1]), True)
    for t in ORDER_A:
        if t[0] == "s": pick_scales(int(t[1]), int(t[-1]), False)
        elif t[0] == "e": evict(int(t[1]), int(t[2]), False)
        elif t[0] == "y": take_y(int(t[1]), False)
    for t in ORDER_P:
        (products_w if t[0] == "w" else product_v)(int(t[1]))

    for s, t, a in ((S.ya, S.sta, 0), (S.yb, S.stb, 2 * EC)):
        Y.wait_ge(s, 2)
        Y.dma_start(T.y[:, a:a + 2 * EC], T.yo[:, a:a + 2 * EC]).then_inc(t, 16)
    Y.wait_ge(S.sta, 16)
    Y.wait_ge(S.stb, 16)
